import numpy as np
import ml_dtypes

BF16 = ml_dtypes.bfloat16


def bf(x):
    return np.asarray(x, np.float32).astype(BF16)


def f32(x):
    return np.asarray(x, np.float32)


def f64(x):
    return np.asarray(x).astype(np.float64)


def striped(idx):
    return np.concatenate([l.reshape(-1, 16).T for l in idx])


def rows(idx, k):
    return np.tile(np.repeat(idx, 16, axis=0), (k // (16 * 8), 1))


def look(tab, idx):
    return np.take_along_axis(f64(tab), rows(idx, len(tab)), axis=1)


K, S, D, V, N = 128, 2048, 2, 512, 1024


def setup_inputs():
    return {"tab": f32(np.random.standard_normal((K, S))), "x0": f32(np.random.standard_normal((K, V))), "offs": striped(np.stack([np.random.permutation(S)[:N] for _ in range(8)]))}


def reference(tab, x0, offs):
    idx = np.stack([g.T.reshape(-1) for g in np.split(offs, 8)])
    x = f64(x0)
    for d in range(D):
        x = np.minimum(x, look(tab, idx[:, d * V:(d + 1) * V]))
    return x

import concourse.mybir as mybir

P = 128
S = 2048
V = 512
D = 2
PER_COLUMN = 16
K = V // PER_COLUMN

FLOPS = D * P * V


def tile_lookup_pool_min_out_kernel(tc, tab, x0, offs, out):
    nc = tc.nc
    f32 = mybir.dt.float32
    with tc.tile_pool(name="held", bufs=1) as held:
        offsets = held.tile([P, D * K], mybir.dt.uint16, name="offsets")
        table = held.tile([P, S], f32, name="table")
        centre = held.tile([P, V], f32, name="centre")
        nc.sync.dma_start(offsets[:], offs)
        nc.sync.dma_start(table[:], tab)
        nc.sync.dma_start(centre[:], x0)

        smallest = centre
        for d in range(D):
            looked_up = table[:].indirect(offsets[:, d * K : (d + 1) * K])
            pooled = held.tile([P, V], f32, name=f"pooled{d}")
            nc.vector.tensor_tensor(pooled[:], looked_up, smallest[:], mybir.AluOpType.min)
            smallest = pooled

        nc.sync.dma_start(out, smallest[:])
